import numpy as np
import ml_dtypes


def mxq(x, axis, fmt="e4m3"):
    dtype, down = {"e4m3": (ml_dtypes.float8_e4m3fn, 7), "e5m2": (ml_dtypes.float8_e5m2, 14)}[fmt]
    v = np.moveaxis(np.asarray(x, np.float32).astype(ml_dtypes.bfloat16).astype(np.float64), axis, -1)
    blocks = v.reshape(v.shape[:-1] + (-1, 32))
    amax = np.abs(blocks).max(-1, keepdims=True)
    byte = np.maximum(np.where(amax > 0, np.frexp(amax)[1] - 1 + 127, 0) - down, 1)
    scale = np.exp2(byte - 127.0)
    codes = (blocks / scale).astype(np.float32).astype(dtype).astype(np.float64)
    return np.moveaxis((codes * scale).reshape(v.shape), -1, axis)


WIDE = False


def mx_kscale(k):
    if not WIDE:
        return np.ones(k)
    levels = np.array([10, -10, 5, -5, 0])
    if k % 512:
        return np.exp2(np.random.permutation(np.resize(levels, k // 32))).repeat(32)
    a = np.empty((k // 512, 16))
    for p in range(k // 512):
        a[p, :8] = np.random.permutation(np.resize(levels, 8))
        for g in range(8):
            far = levels[np.abs(levels - a[p, g]) >= 10]
            a[p, g + 8] = far[np.random.randint(len(far))]
    return np.exp2(a.ravel()).repeat(32)


def f64(x):
    return np.asarray(x).astype(np.float64)


def striped(idx):
    return np.tile(idx.reshape(-1, 16).T, (8, 1)).astype(np.uint16)


def unstriped(offs):
    return offs[:16].T.reshape(-1).astype(np.int64)


E2M1 = np.array([0.0, 0.5, 1.0, 1.5, 2.0, 3.0, 4.0, 6.0, -0.0, -0.5, -1.0, -1.5, -2.0, -3.0, -4.0, -6.0])


def pack_weight(w, fmt):
    k, n = w.shape
    w = f64(np.asarray(w, np.float32).astype(ml_dtypes.bfloat16)).reshape(k // 32, 32, n)
    amax = np.abs(w).max(1)
    if fmt == "e4m3":
        byte = np.frexp(amax)[1] - 1 + 127 - 7
    else:
        mant, ex = np.frexp(amax / 6.0)
        byte = np.where(mant > 0.5, ex, ex - 1) + 127
    byte = np.clip(np.where(amax > 0, byte, 1), 1, 254)
    scaled = (w * np.exp2(127.0 - byte)[:, None, :]).reshape(k, n).astype(np.float32)
    by_word = np.ascontiguousarray(scaled.reshape(k // 512, 128, 4, n).transpose(0, 1, 3, 2))
    if fmt == "e4m3":
        words = by_word.astype(ml_dtypes.float8_e4m3fn).view(np.uint8)
    else:
        c = by_word.astype(ml_dtypes.float4_e2m1fn).view(np.uint8) & 0xF
        words = (c[..., 0::2] | (c[..., 1::2] << 4)).reshape(k // 512, 128, 2 * n)
    return np.ascontiguousarray(words), np.ascontiguousarray(byte.astype(np.uint8).reshape(k // 512, 16, n))


def unpack_weight(words, scales, fmt):
    g, _, n = scales.shape
    words = np.ascontiguousarray(words).reshape(g, 128, n, -1)
    if fmt == "e4m3":
        vals = words.view(ml_dtypes.float8_e4m3fn).astype(np.float64)
    else:
        nib = np.empty((g, 128, n, 4), np.uint8)
        nib[..., 0::2] = words & 0xF
        nib[..., 1::2] = words >> 4
        vals = E2M1[nib]
    vals = vals * np.repeat(np.exp2(scales.astype(np.float64) - 127.0), 8, axis=1)[..., None]
    return vals.transpose(0, 1, 3, 2).reshape(g * 512, n)


def gelu(v):
    return 0.5 * v * (1.0 + np.tanh(np.sqrt(2.0 / np.pi) * (v + 0.044715 * v**3)))


K, KU, KR, T, S, H, P, N = 1536, 1024, 512, 2048, 1024, 512, 512, 768

def setup_inputs():
    n = np.random.standard_normal
    s = mx_kscale(K)[:, None]
    u = mx_kscale(H)[:, None]
    tab_words, tab_scales = pack_weight(n((K, T)) * s, "e4m3")
    w4_words, w4_scales = pack_weight(n((KR, H)) / np.sqrt(K) / s[KU:] * 1.4, "e2m1")
    wd_words, wd_scales = pack_weight(n((K, H)) / np.sqrt(K) / s * 1.5, "e4m3")
    wb_words, wb_scales = pack_weight(n((H, N)) / np.sqrt(H) / u, "e2m1")
    return {
        "tab_words": tab_words, "tab_scales": tab_scales,
        "offs": striped(np.random.permutation(T)[:S]),
        "pos1": striped(np.random.permutation(S)[:P]),
        "pos2": striped(np.random.permutation(S)[:P]),
        "w1": (n((KU, H)) / np.sqrt(K) / s[:KU]).astype(np.float32),
        "w4_words": w4_words, "w4_scales": w4_scales,
        "wd_words": wd_words, "wd_scales": wd_scales,
        "gain": (2.0 * np.exp(0.3 * n(H)) * u[:, 0]).astype(np.float32),
        "base": (0.8 * n((H, P)) * u).astype(np.float32),
        "tail": np.exp(0.4 * n(H)).astype(np.float32),
        "wa": (n((H, N)) / np.sqrt(H) / u).astype(np.float32),
        "wb_words": wb_words, "wb_scales": wb_scales,
    }

def reference(tab_words, tab_scales, offs, pos1, pos2, w1, w4_words, w4_scales,
              wd_words, wd_scales, gain, base, tail, wa, wb_words, wb_scales):
    v = unpack_weight(tab_words, tab_scales, "e4m3")[:, unstriped(offs)]
    w4 = unpack_weight(w4_words, w4_scales, "e2m1")
    wd = unpack_weight(wd_words, wd_scales, "e4m3")
    wb = unpack_weight(wb_words, wb_scales, "e2m1")
    a = mxq(f64(w1), 0, "e4m3").T @ v[:KU] + w4.T @ v[KU:]
    d = wd.T @ v
    h = a / (1.0 + np.abs(d)) * f64(gain)[:, None]
    xa = h[:, unstriped(pos1)] + f64(base)
    xb = h[:, unstriped(pos2)] * f64(tail)[:, None]
    ya = mxq(f64(wa), 0, "e4m3").T @ mxq(xa, 0, "e4m3")
    yb = wb.T @ mxq(xb, 0, "e4m3")
    return np.maximum(ya, yb)

@@ -1,0 +1,292 @@
+from contextlib import ExitStack
+
+import concourse.mybir as mybir
+
+F32 = mybir.dt.float32
+BF16 = mybir.dt.bfloat16
+I32 = mybir.dt.int32
+U32 = mybir.dt.uint32
+U16 = mybir.dt.uint16
+U8 = mybir.dt.uint8
+FP8X4 = mybir.dt.float8_e4m3fn_x4
+FP4X4 = mybir.dt.float4_e2m1fn_x4
+ACT = mybir.ActivationFunctionType
+ALU = mybir.AluOpType
+
+P = 128
+PACK = 4
+T = 2048
+S = 1024
+H = 512
+J = 512
+N = 768
+BANK = 512
+PASSES = 3
+JH = J // 2
+FLOPS = 2 * (2 * 1536 * H * S + 2 * H * N * J)
+
+
+def tile_list_tracer_release_scores_kernel(
+    tc, tab_words, tab_scales, offs, pos1, pos2, w1, w4_words, w4_scales,
+    wd_words, wd_scales, gain, base, tail, wa, wb_words, wb_scales, out,
+):
+    nc = tc.nc
+    with ExitStack() as ctx:
+        sb = ctx.enter_context(tc.tile_pool(name="sb", bufs=1))
+        psum = ctx.enter_context(tc.psum_pool(name="psum", bufs=1))
+
+        def tile(name, shape, dtype, tag=None):
+            return sb.tile(shape, dtype, name=name, tag=tag or name, align_bytes=64)
+
+        tab_sc = tile("tab_sc", [P, T], U8)
+        wd_sc_raw = tile("wd_sc_raw", [P, H], U8)
+        w4_sc_raw = tile("w4_sc_raw", [P, H], U8)
+        wb_sc = tile("wb_sc", [P, N], U8)
+        for plane in (tab_sc, wd_sc_raw, w4_sc_raw, wb_sc):
+            nc.vector.memset(plane[:].bitcast(I32), 0)
+
+        idx = sb.tile([P, S // 16], U16, name="idx")
+        p1 = sb.tile([P, J // 16], U16, name="p1")
+        p2 = sb.tile([P, J // 16], U16, name="p2")
+        nc.sync.dma_start(idx[:], offs)
+        nc.sync.dma_start(p1[:], pos1)
+        nc.sync.dma_start(p2[:], pos2)
+        w4_raw = tile("w4_raw", [P, 2 * H], U8)
+        nc.gpsimd.dma_start(w4_raw[:].bitcast(I32), w4_words[0].bitcast(I32))
+
+        def load_tab(a, tag):
+            words = tile("tab%d" % a, [P, T], I32, tag=tag)
+            nc.sync.dma_start(words[:], tab_words[a].rearrange("p t i -> p (t i)").bitcast(I32))
+            return words
+
+        def load_w1(g, tag):
+            raw = tile("w1_raw%d" % g, [P, PACK, H], F32, tag=tag)
+            nc.sync.dma_start(raw[:], w1[512 * g : 512 * (g + 1), :].rearrange("(p j) c -> p j c", j=PACK))
+            return raw
+
+        def load_scale_rows(engine, plane, first, scales):
+            rows = 4 * scales.shape[0]
+            for q in range(4):
+                engine.dma_start(
+                    plane[32 * q + first : 32 * q + first + rows, :].bitcast(I32),
+                    scales.bitcast(I32)[:, 4 * q : 4 * q + 4, :],
+                )
+
+        tab0 = load_tab(0, "slot_a")
+        wd_raw = tile("wd_raw", [P, PASSES, H], I32, tag="slot_b")
+        nc.sync.dma_start(wd_raw[:], wd_words.rearrange("a p c i -> p a (c i)").bitcast(I32))
+        load_scale_rows(nc.scalar, tab_sc, 4, tab_scales[0:2])
+        load_scale_rows(nc.scalar, tab_sc, 0, tab_scales[2:3])
+        load_scale_rows(nc.gpsimd, wd_sc_raw, 4, wd_scales)
+        load_scale_rows(nc.scalar, w4_sc_raw, 0, w4_scales)
+        gain_sb = tile("gain_sb", [P, PACK], F32)
+        tail_sb = tile("tail_sb", [P, PACK], F32)
+        nc.gpsimd.dma_start(gain_sb[:], gain.rearrange("(p t) -> p t", t=PACK))
+        nc.gpsimd.dma_start(tail_sb[:], tail.rearrange("(p t) -> p t", t=PACK))
+        load_scale_rows(nc.gpsimd, wb_sc, 0, wb_scales)
+
+        w4_w = tile("w4_w", [P, 2 * H], U8)
+        nc.vector.tensor_copy(
+            out=w4_w[:].rearrange("p (t m b) -> p m t b", t=PACK, b=2),
+            in_=w4_raw[:].rearrange("p (m t b) -> p m t b", t=PACK, b=2),
+        )
+        tab1 = load_tab(1, "w4_raw")
+
+        half_cols = BANK // 16
+
+        def gather_table(name, window, dtype):
+            picked = []
+            for h in range(2):
+                part = tile("%s_%d" % (name, h), [P, BANK], dtype)
+                nc.vector.tensor_copy(part[:], window.indirect(idx[:, h * half_cols : (h + 1) * half_cols]))
+                picked.append(part)
+            return picked
+
+        def deal_scales(name, raw):
+            dealt = tile(name, [P, H], U8)
+            nc.vector.tensor_copy(
+                out=dealt[:].rearrange("p (t m) -> p m t", t=PACK),
+                in_=raw[:].rearrange("p (m t) -> p m t", t=PACK),
+            )
+            return dealt
+
+        v_w = [gather_table("v0", tab0[:].bitcast(U32), U32)]
+        w1_raw0 = load_w1(0, "slot_a")
+        wd_w = tile("wd_w", [P, PASSES, H], I32)
+        nc.vector.tensor_copy(
+            out=wd_w[:].rearrange("p a (t u i) -> p a u t i", t=PACK, i=4),
+            in_=wd_raw[:].rearrange("p a (u i t) -> p a u t i", t=PACK, i=4),
+        )
+        tab2 = load_tab(2, "slot_b")
+        v_sc = gather_table("v_sc", tab_sc[:], U8)
+        wd_sc = deal_scales("wd_sc", wd_sc_raw)
+        v_w.append(gather_table("v1", tab1[:].bitcast(U32), U32))
+        w1_raw1 = load_w1(1, "w4_raw")
+        v_w.append(gather_table("v2", tab2[:].bitcast(U32), U32))
+        v_row = (4, 8, 0)
+        wd_row = (4, 8, 12)
+
+        def bank(b, name):
+            return psum.tile([P, BANK], F32, name=name, tag="bank%d" % b)
+
+        def banks(pair, name):
+            return [bank(2 * pair + h, "%s_%d" % (name, h)) for h in range(2)]
+
+        def d_pass(ps, t, h, a):
+            cols = slice(P * t, P * (t + 1))
+            nc.tensor.matmul_mx(
+                ps[h][:], lhsT=wd_w[:, a, cols].bitcast(FP8X4), lhsT_scale=wd_sc[wd_row[a] :, cols],
+                rhs=v_w[a][h][:].bitcast(FP8X4), rhs_scale=v_sc[h][v_row[a] :, :],
+                start=(a == 0), stop=(a == PASSES - 1),
+            )
+
+        d_ps = {0: banks(0, "d0"), 1: banks(1, "d1")}
+        for a in range(PASSES):
+            for h in range(2):
+                for t in range(2):
+                    d_pass(d_ps[t], t, h, a)
+
+        w1_q = [tile("w1_q%d" % g, [P, H], U32) for g in range(2)]
+        w1_sc = [tile("w1_sc%d" % g, [P, H], U8) for g in range(2)]
+        w1_bf = [tile("w1_bf%d" % g, [P, PACK * H], BF16) for g in range(2)]
+        for g, (copy, raw) in enumerate(((nc.scalar.copy, w1_raw0), (nc.vector.tensor_copy, w1_raw1))):
+            copy(
+                w1_bf[g][:].rearrange("p (t m j) -> p m j t", t=PACK, j=PACK),
+                raw[:].rearrange("p j (m t) -> p m j t", t=PACK),
+            )
+        wa_raw = tile("wa_raw", [P, PACK, N], F32, tag="slot_a")
+        nc.sync.dma_start(wa_raw[:], wa.rearrange("(p j) n -> p j n", j=PACK))
+        base_sb = tile("base_sb", [P, PACK, J], F32, tag="slot_b")
+        nc.sync.dma_start(base_sb[:], base.rearrange("(p t) j -> p t j", t=PACK))
+        wb_w = tile("wb_w", [P, 2 * N], U8, tag="w4_raw")
+        nc.sync.dma_start(wb_w[:].bitcast(I32), wb_words[0].bitcast(I32))
+        w4_sc = deal_scales("w4_sc", w4_sc_raw)
+        nc.vector.quantize_mx(out=w1_q[0][:].bitcast(FP8X4), scales=w1_sc[0][:], in_=w1_bf[0][:])
+        for t in range(PACK):
+            cols = slice(P * t, P * (t + 1))
+            nc.vector.quantize_mx(out=w1_q[1][:, cols].bitcast(FP8X4), scales=w1_sc[1][:, cols], in_=w1_bf[1][:, H * t : H * (t + 1)])
+
+        def d_sum(t, pair):
+            d_ps[t] = banks(pair, "d%d" % t)
+            for h in range(2):
+                for a in range(PASSES):
+                    d_pass(d_ps[t], t, h, a)
+
+        def a_sum(t, pair):
+            cols = slice(P * t, P * (t + 1))
+            ps = banks(pair, "a%d" % t)
+
+            def w1_pass(g, h):
+                nc.tensor.matmul_mx(
+                    ps[h][:], lhsT=w1_q[g][:, cols].bitcast(FP8X4), lhsT_scale=w1_sc[g][:, cols],
+                    rhs=v_w[g][h][:].bitcast(FP8X4), rhs_scale=v_sc[h][v_row[g] :, :],
+                    start=(g == 0), stop=(g == 1),
+                )
+
+            for h in range(2):
+                w1_pass(0, h)
+                nc.tensor.matmul_mx(
+                    ps[h][:], lhsT=w4_w[:, 2 * P * t : 2 * P * (t + 1)].bitcast(FP4X4), lhsT_scale=w4_sc[:, cols],
+                    rhs=v_w[2][h][:].bitcast(FP8X4), rhs_scale=v_sc[h][:, :],
+                    start=False, stop=False,
+                )
+            for h in range(2):
+                w1_pass(1, h)
+            return ps
+
+        ga = tile("ga", [P, PACK, J], F32)
+        gb = tile("gb", [P, PACK, J], F32)
+        a_pair = (3, 1, 2, 3)
+        d_pair = (0, 1, 2, 0)
+        for t in range(PACK):
+            mag = [sb.tile([P, BANK], F32, name="mag", bufs=4) for h in range(2)]
+            root = [sb.tile([P, BANK], F32, name="root", bufs=4) for h in range(2)]
+            damp = [tile("damp%d_%d" % (t, h), [P, BANK], F32) for h in range(2)]
+            for h in range(2):
+                nc.scalar.activation(mag[h][:], d_ps[t][h][:], ACT.Abs)
+            for h in range(2):
+                nc.scalar.activation(root[h][:], mag[h][:], ACT.Abs_reciprocal_sqrt, bias=1.0)
+            for h in range(2):
+                nc.scalar.activation(damp[h][:], root[h][:], ACT.Square)
+            a_ps = a_sum(t, a_pair[t])
+            if t + 2 < PACK:
+                d_sum(t + 2, d_pair[t + 2])
+            h_sb = tile("h%d" % t, [P, S], F32)
+            for h in range(2):
+                nc.vector.scalar_tensor_tensor(
+                    out=h_sb[:, h * BANK : (h + 1) * BANK], in0=a_ps[h][:], scalar=gain_sb[:, t : t + 1],
+                    in1=damp[h][:], op0=ALU.mult, op1=ALU.mult,
+                )
+            nc.vector.tensor_copy(gb[:, t, :], h_sb[:].indirect(p2[:]))
+            nc.vector.tensor_copy(ga[:, t, :], h_sb[:].indirect(p1[:]))
+
+        wa_bf = tile("wa_bf", [P, PACK * N], BF16)
+        wa_q = tile("wa_q", [P, N], U32)
+        wa_sc = tile("wa_sc", [P, N], U8)
+        for c0 in range(0, N, 256):
+            nc.scalar.copy(
+                out=wa_bf[:, PACK * c0 : PACK * (c0 + 256)].rearrange("p (c i j) -> p c j i", i=4, j=PACK),
+                in_=wa_raw[:, :, c0 : c0 + 256].rearrange("p j (c i) -> p c j i", i=4),
+            )
+        for c0 in range(0, N, 256):
+            nc.vector.quantize_mx(out=wa_q[:, c0 : c0 + 256].bitcast(FP8X4), scales=wa_sc[:, c0 : c0 + 256], in_=wa_bf[:, PACK * c0 : PACK * (c0 + 256)])
+
+        def woven(x):
+            return x[:].rearrange("p (c i t) -> p c t i", i=4, t=PACK)
+
+        def by_line(x, half):
+            return x[:, :, JH * half : JH * (half + 1)].rearrange("p t (c i) -> p c t i", i=4)
+
+        def quantized(name, x_bf):
+            codes = tile(name + "_q", [P, JH], U32)
+            scales = tile(name + "_sc", [P, JH], U8)
+            nc.vector.quantize_mx(out=codes[:].bitcast(FP8X4), scales=scales[:], in_=x_bf[:])
+            return codes, scales
+
+        xa_bf = [tile("xa_bf%d" % half, [P, PACK * JH], BF16) for half in range(2)]
+        xb_bf = [tile("xb_bf%d" % half, [P, PACK * JH], BF16) for half in range(2)]
+        xb_rows = tile("xb_rows", [P, PACK, JH], BF16)
+        for t in range(PACK):
+            nc.scalar.activation(xb_rows[:, t, :], gb[:, t, JH:], ACT.Copy, scale=tail_sb[:, t : t + 1])
+        nc.scalar.copy(out=woven(xb_bf[1]), in_=by_line(xb_rows, 0))
+        nc.vector.tensor_tensor(
+            out=woven(xb_bf[0]), in0=by_line(gb, 0),
+            in1=tail_sb[:].unsqueeze(1).unsqueeze(3).to_broadcast([P, JH // 4, PACK, 4]), op=ALU.mult,
+        )
+        nc.vector.tensor_tensor(out=woven(xa_bf[0]), in0=by_line(ga, 0), in1=by_line(base_sb, 0), op=ALU.add)
+        xb_q = [quantized("xb0", xb_bf[0])]
+        xa_q = [quantized("xa0", xa_bf[0])]
+        nc.vector.tensor_tensor(out=woven(xa_bf[1]), in0=by_line(ga, 1), in1=by_line(base_sb, 1), op=ALU.add)
+        xb_q.append(quantized("xb1", xb_bf[1]))
+        xa_q.append(quantized("xa1", xa_bf[1]))
+
+        def score(kind, half, pair, b):
+            ps = bank(b, "y%s%d_%d" % (kind, half, pair))
+            for e in range(2):
+                n = 2 * pair + e
+                cols = slice(P * n, P * (n + 1))
+                if kind == "a":
+                    lhsT, lhsT_scale, (codes, scales) = wa_q[:, cols].bitcast(FP8X4), wa_sc[:, cols], xa_q[half]
+                else:
+                    lhsT, lhsT_scale, (codes, scales) = wb_w[:, 2 * P * n : 2 * P * (n + 1)].bitcast(FP4X4), wb_sc[:, cols], xb_q[half]
+                nc.tensor.matmul_mx(
+                    ps[:, JH * e : JH * (e + 1)], lhsT=lhsT, lhsT_scale=lhsT_scale,
+                    rhs=codes[:].bitcast(FP8X4), rhs_scale=scales[:], start=True, stop=True,
+                )
+            return ps
+
+        for half in range(2):
+            yb_sb = []
+            for pair in range(3):
+                yb_ps = score("b", half, pair, (6 * half + pair) % 8)
+                copied = tile("yb_sb%d_%d" % (half, pair), [P, BANK], F32)
+                nc.scalar.copy(out=copied[:], in_=yb_ps[:])
+                yb_sb.append(copied)
+            for pair in range(3):
+                ya_ps = score("a", half, pair, (6 * half + 3 + pair) % 8)
+                res = tile("res%d_%d" % (half, pair), [P, BANK], F32)
+                nc.vector.tensor_tensor(out=res[:], in0=ya_ps[:], in1=yb_sb[pair][:], op=ALU.max)
+                nc.sync.dma_start(
+                    out[2 * P * pair : 2 * P * (pair + 1), JH * half : JH * (half + 1)].rearrange("(e p) j -> p e j", p=P),
+                    res[:].rearrange("p (e j) -> p e j", e=2),
+                )

@@ -33,34 +33,31 @@ def tile_list_tracer_release_scores_kernel(
     nc = tc.nc
     with ExitStack() as ctx:
         sb = ctx.enter_context(tc.tile_pool(name="sb", bufs=1))
+        shared = ctx.enter_context(tc.tile_pool(name="shared", bufs=1))
         psum = ctx.enter_context(tc.psum_pool(name="psum", bufs=1))
 
-        def tile(name, shape, dtype, tag=None):
+        def tile(name, shape, dtype, tag=None, offset=None):
+            if offset is not None:
+                return shared.tile(shape, dtype, name=name, align_bytes=64, offset=offset)
             return sb.tile(shape, dtype, name=name, tag=tag or name, align_bytes=64)
 
         tab_sc = tile("tab_sc", [P, T], U8)
         wd_sc_raw = tile("wd_sc_raw", [P, H], U8)
         w4_sc_raw = tile("w4_sc_raw", [P, H], U8)
         wb_sc = tile("wb_sc", [P, N], U8)
-        for plane in (tab_sc, wd_sc_raw, w4_sc_raw, wb_sc):
+        v2_sc = tile("v2_sc", [P, S], U8)
+        for plane in (tab_sc, v2_sc):
             nc.vector.memset(plane[:].bitcast(I32), 0)
+        for plane in (wd_sc_raw, w4_sc_raw, wb_sc):
+            nc.gpsimd.memset(plane[:].bitcast(I32), 0)
 
-        idx = sb.tile([P, S // 16], U16, name="idx")
-        p1 = sb.tile([P, J // 16], U16, name="p1")
-        p2 = sb.tile([P, J // 16], U16, name="p2")
-        nc.sync.dma_start(idx[:], offs)
-        nc.sync.dma_start(p1[:], pos1)
-        nc.sync.dma_start(p2[:], pos2)
-        w4_raw = tile("w4_raw", [P, 2 * H], U8)
-        nc.gpsimd.dma_start(w4_raw[:].bitcast(I32), w4_words[0].bitcast(I32))
-
-        def load_tab(a, tag):
-            words = tile("tab%d" % a, [P, T], I32, tag=tag)
+        def load_tab(a, **place):
+            words = tile("tab%d" % a, [P, T], I32, **place)
             nc.sync.dma_start(words[:], tab_words[a].rearrange("p t i -> p (t i)").bitcast(I32))
             return words
 
-        def load_w1(g, tag):
-            raw = tile("w1_raw%d" % g, [P, PACK, H], F32, tag=tag)
+        def load_w1(g, **place):
+            raw = tile("w1_raw%d" % g, [P, PACK, H], F32, **place)
             nc.sync.dma_start(raw[:], w1[512 * g : 512 * (g + 1), :].rearrange("(p j) c -> p j c", j=PACK))
             return raw
 
@@ -72,17 +69,28 @@ def tile_list_tracer_release_scores_kernel(
                     scales.bitcast(I32)[:, 4 * q : 4 * q + 4, :],
                 )
 
-        tab0 = load_tab(0, "slot_a")
-        wd_raw = tile("wd_raw", [P, PASSES, H], I32, tag="slot_b")
+        idx = sb.tile([P, S // 16], U16, name="idx")
+        p1 = sb.tile([P, J // 16], U16, name="p1")
+        p2 = sb.tile([P, J // 16], U16, name="p2")
+        w4_raw = tile("w4_raw", [P, 2 * H], U8)
+        nc.sync.dma_start(w4_raw[:].bitcast(I32), w4_words[0].bitcast(I32))
+        tab0 = load_tab(0)
+        nc.sync.dma_start(idx[:], offs)
+        nc.sync.dma_start(p1[:], pos1)
+        wd_raw = tile("wd_raw", [P, PASSES, H], I32, offset=4 * T)
         nc.sync.dma_start(wd_raw[:], wd_words.rearrange("a p c i -> p a (c i)").bitcast(I32))
-        load_scale_rows(nc.scalar, tab_sc, 4, tab_scales[0:2])
-        load_scale_rows(nc.scalar, tab_sc, 0, tab_scales[2:3])
-        load_scale_rows(nc.gpsimd, wd_sc_raw, 4, wd_scales)
-        load_scale_rows(nc.scalar, w4_sc_raw, 0, w4_scales)
-        gain_sb = tile("gain_sb", [P, PACK], F32)
-        tail_sb = tile("tail_sb", [P, PACK], F32)
-        nc.gpsimd.dma_start(gain_sb[:], gain.rearrange("(p t) -> p t", t=PACK))
-        nc.gpsimd.dma_start(tail_sb[:], tail.rearrange("(p t) -> p t", t=PACK))
+        nc.sync.dma_start(p2[:], pos2)
+        tab1 = load_tab(1)
+        w1_raw0 = load_w1(0)
+        tab2 = load_tab(2, offset=0)
+        w1_raw1 = load_w1(1)
+        load_scale_rows(nc.scalar, tab_sc, 0, tab_scales)
+        load_scale_rows(nc.gpsimd, wd_sc_raw, 0, wd_scales)
+        ones = tile("ones", [P, 1], F32)
+        warm = tile("warm", [P, 1], F32)
+        nc.gpsimd.memset(ones[:], 1.0)
+        nc.scalar.activation(warm[:], ones[:], ACT.Abs_reciprocal_sqrt)
+        load_scale_rows(nc.gpsimd, w4_sc_raw, 0, w4_scales)
         load_scale_rows(nc.gpsimd, wb_sc, 0, wb_scales)
 
         w4_w = tile("w4_w", [P, 2 * H], U8)
@@ -90,20 +98,20 @@ def tile_list_tracer_release_scores_kernel(
             out=w4_w[:].rearrange("p (t m b) -> p m t b", t=PACK, b=2),
             in_=w4_raw[:].rearrange("p (m t b) -> p m t b", t=PACK, b=2),
         )
-        tab1 = load_tab(1, "w4_raw")
 
         half_cols = BANK // 16
 
-        def gather_table(name, window, dtype):
-            picked = []
+        def half(h):
+            return slice(h * BANK, (h + 1) * BANK)
+
+        def gather_table(name, window, dtype, **place):
+            picked = tile(name, [P, S], dtype, **place)
             for h in range(2):
-                part = tile("%s_%d" % (name, h), [P, BANK], dtype)
-                nc.vector.tensor_copy(part[:], window.indirect(idx[:, h * half_cols : (h + 1) * half_cols]))
-                picked.append(part)
+                nc.vector.tensor_copy(picked[:, half(h)], window.indirect(idx[:, h * half_cols : (h + 1) * half_cols]))
             return picked
 
-        def deal_scales(name, raw):
-            dealt = tile(name, [P, H], U8)
+        def deal_scales(name, raw, **place):
+            dealt = tile(name, [P, H], U8, **place)
             nc.vector.tensor_copy(
                 out=dealt[:].rearrange("p (t m) -> p m t", t=PACK),
                 in_=raw[:].rearrange("p (m t) -> p m t", t=PACK),
@@ -111,20 +119,21 @@ def tile_list_tracer_release_scores_kernel(
             return dealt
 
         v_w = [gather_table("v0", tab0[:].bitcast(U32), U32)]
-        w1_raw0 = load_w1(0, "slot_a")
         wd_w = tile("wd_w", [P, PASSES, H], I32)
         nc.vector.tensor_copy(
             out=wd_w[:].rearrange("p a (t u i) -> p a u t i", t=PACK, i=4),
             in_=wd_raw[:].rearrange("p a (u i t) -> p a u t i", t=PACK, i=4),
         )
-        tab2 = load_tab(2, "slot_b")
-        v_sc = gather_table("v_sc", tab_sc[:], U8)
-        wd_sc = deal_scales("wd_sc", wd_sc_raw)
-        v_w.append(gather_table("v1", tab1[:].bitcast(U32), U32))
-        w1_raw1 = load_w1(1, "w4_raw")
+        v_sc = gather_table("v_sc", tab_sc[:], U8, offset=4 * T + H)
+        for q in range(4):
+            nc.scalar.dma_start(v2_sc[32 * q : 32 * q + 4, :].bitcast(I32), v_sc[32 * q + 8 : 32 * q + 12, :].bitcast(I32))
+        gain_sb = tile("gain_sb", [P, PACK], F32, tag="tab_sc")
+        nc.sync.dma_start(gain_sb[:], gain.rearrange("(p t) -> p t", t=PACK))
+        wd_sc = deal_scales("wd_sc", wd_sc_raw, offset=4 * T)
+        v_w.append(gather_table("v1", tab1[:].bitcast(U32), U32, tag="wd_sc_raw"))
+        wa_raw = tile("wa_raw", [P, PACK, N], F32, tag="tab1")
+        nc.sync.dma_start(wa_raw[:], wa.rearrange("(p j) n -> p j n", j=PACK))
         v_w.append(gather_table("v2", tab2[:].bitcast(U32), U32))
-        v_row = (4, 8, 0)
-        wd_row = (4, 8, 12)
 
         def bank(b, name):
             return psum.tile([P, BANK], F32, name=name, tag="bank%d" % b)
@@ -135,18 +144,18 @@ def tile_list_tracer_release_scores_kernel(
         def d_pass(ps, t, h, a):
             cols = slice(P * t, P * (t + 1))
             nc.tensor.matmul_mx(
-                ps[h][:], lhsT=wd_w[:, a, cols].bitcast(FP8X4), lhsT_scale=wd_sc[wd_row[a] :, cols],
-                rhs=v_w[a][h][:].bitcast(FP8X4), rhs_scale=v_sc[h][v_row[a] :, :],
+                ps[h][:], lhsT=wd_w[:, a, cols].bitcast(FP8X4), lhsT_scale=wd_sc[4 * a :, cols],
+                rhs=v_w[a][:, half(h)].bitcast(FP8X4), rhs_scale=v_sc[4 * a :, half(h)],
                 start=(a == 0), stop=(a == PASSES - 1),
             )
 
         d_ps = {0: banks(0, "d0"), 1: banks(1, "d1")}
-        for a in range(PASSES):
+        for t in range(2):
             for h in range(2):
-                for t in range(2):
+                for a in range(PASSES):
                     d_pass(d_ps[t], t, h, a)
 
-        w1_q = [tile("w1_q%d" % g, [P, H], U32) for g in range(2)]
+        w1_q = [tile("w1_q0", [P, H], U32, offset=0), tile("w1_q1", [P, H], U32)]
         w1_sc = [tile("w1_sc%d" % g, [P, H], U8) for g in range(2)]
         w1_bf = [tile("w1_bf%d" % g, [P, PACK * H], BF16) for g in range(2)]
         for g, (copy, raw) in enumerate(((nc.scalar.copy, w1_raw0), (nc.vector.tensor_copy, w1_raw1))):
@@ -154,13 +163,13 @@ def tile_list_tracer_release_scores_kernel(
                 w1_bf[g][:].rearrange("p (t m j) -> p m j t", t=PACK, j=PACK),
                 raw[:].rearrange("p j (m t) -> p m j t", t=PACK),
             )
-        wa_raw = tile("wa_raw", [P, PACK, N], F32, tag="slot_a")
-        nc.sync.dma_start(wa_raw[:], wa.rearrange("(p j) n -> p j n", j=PACK))
-        base_sb = tile("base_sb", [P, PACK, J], F32, tag="slot_b")
+        w4_sc = deal_scales("w4_sc", w4_sc_raw, offset=4 * H)
+        base_sb = tile("base_sb", [P, PACK, J], F32, tag="w1_raw0")
         nc.sync.dma_start(base_sb[:], base.rearrange("(p t) j -> p t j", t=PACK))
-        wb_w = tile("wb_w", [P, 2 * N], U8, tag="w4_raw")
+        tail_sb = tile("tail_sb", [P, PACK], F32, tag="w1_raw1")
+        nc.sync.dma_start(tail_sb[:], tail.rearrange("(p t) -> p t", t=PACK))
+        wb_w = tile("wb_w", [P, 2 * N], U8, tag="w4_sc_raw")
         nc.sync.dma_start(wb_w[:].bitcast(I32), wb_words[0].bitcast(I32))
-        w4_sc = deal_scales("w4_sc", w4_sc_raw)
         nc.vector.quantize_mx(out=w1_q[0][:].bitcast(FP8X4), scales=w1_sc[0][:], in_=w1_bf[0][:])
         for t in range(PACK):
             cols = slice(P * t, P * (t + 1))
@@ -179,28 +188,26 @@ def tile_list_tracer_release_scores_kernel(
             def w1_pass(g, h):
                 nc.tensor.matmul_mx(
                     ps[h][:], lhsT=w1_q[g][:, cols].bitcast(FP8X4), lhsT_scale=w1_sc[g][:, cols],
-                    rhs=v_w[g][h][:].bitcast(FP8X4), rhs_scale=v_sc[h][v_row[g] :, :],
-                    start=(g == 0), stop=(g == 1),
+                    rhs=v_w[g][:, half(h)].bitcast(FP8X4), rhs_scale=v_sc[4 * g :, half(h)],
+                    start=(g == 0), stop=False,
                 )
 
             for h in range(2):
                 w1_pass(0, h)
+                w1_pass(1, h)
                 nc.tensor.matmul_mx(
                     ps[h][:], lhsT=w4_w[:, 2 * P * t : 2 * P * (t + 1)].bitcast(FP4X4), lhsT_scale=w4_sc[:, cols],
-                    rhs=v_w[2][h][:].bitcast(FP8X4), rhs_scale=v_sc[h][:, :],
-                    start=False, stop=False,
+                    rhs=v_w[2][:, half(h)].bitcast(FP8X4), rhs_scale=v2_sc[:, half(h)],
+                    start=False, stop=True,
                 )
-            for h in range(2):
-                w1_pass(1, h)
             return ps
 
         ga = tile("ga", [P, PACK, J], F32)
         gb = tile("gb", [P, PACK, J], F32)
-        a_pair = (3, 1, 2, 3)
-        d_pair = (0, 1, 2, 0)
+        a_pair = (2, 1, 2, 1)
         for t in range(PACK):
             mag = [sb.tile([P, BANK], F32, name="mag", bufs=4) for h in range(2)]
-            root = [sb.tile([P, BANK], F32, name="root", bufs=4) for h in range(2)]
+            root = [tile("root%d_%d" % (t, h), [P, BANK], F32, tag="root%d" % h) for h in range(2)]
             damp = [tile("damp%d_%d" % (t, h), [P, BANK], F32) for h in range(2)]
             for h in range(2):
                 nc.scalar.activation(mag[h][:], d_ps[t][h][:], ACT.Abs)
@@ -209,8 +216,8 @@ def tile_list_tracer_release_scores_kernel(
             for h in range(2):
                 nc.scalar.activation(damp[h][:], root[h][:], ACT.Square)
             a_ps = a_sum(t, a_pair[t])
-            if t + 2 < PACK:
-                d_sum(t + 2, d_pair[t + 2])
+            if t in (0, 2):
+                d_sum(t // 2 + 2, 0)
             h_sb = tile("h%d" % t, [P, S], F32)
             for h in range(2):
                 nc.vector.scalar_tensor_tensor(
@@ -220,7 +227,7 @@ def tile_list_tracer_release_scores_kernel(
             nc.vector.tensor_copy(gb[:, t, :], h_sb[:].indirect(p2[:]))
             nc.vector.tensor_copy(ga[:, t, :], h_sb[:].indirect(p1[:]))
 
-        wa_bf = tile("wa_bf", [P, PACK * N], BF16)
+        wa_bf = tile("wa_bf", [P, PACK * N], BF16, tag="root0")
         wa_q = tile("wa_q", [P, N], U32)
         wa_sc = tile("wa_sc", [P, N], U8)
         for c0 in range(0, N, 256):
@@ -234,8 +241,8 @@ def tile_list_tracer_release_scores_kernel(
         def woven(x):
             return x[:].rearrange("p (c i t) -> p c t i", i=4, t=PACK)
 
-        def by_line(x, half):
-            return x[:, :, JH * half : JH * (half + 1)].rearrange("p t (c i) -> p c t i", i=4)
+        def by_line(x, jh):
+            return x[:, :, JH * jh : JH * (jh + 1)].rearrange("p t (c i) -> p c t i", i=4)
 
         def quantized(name, x_bf):
             codes = tile(name + "_q", [P, JH], U32)
@@ -243,9 +250,9 @@ def tile_list_tracer_release_scores_kernel(
             nc.vector.quantize_mx(out=codes[:].bitcast(FP8X4), scales=scales[:], in_=x_bf[:])
             return codes, scales
 
-        xa_bf = [tile("xa_bf%d" % half, [P, PACK * JH], BF16) for half in range(2)]
-        xb_bf = [tile("xb_bf%d" % half, [P, PACK * JH], BF16) for half in range(2)]
-        xb_rows = tile("xb_rows", [P, PACK, JH], BF16)
+        xa_bf = [tile("xa_bf%d" % jh, [P, PACK * JH], BF16) for jh in range(2)]
+        xb_bf = [tile("xb_bf%d" % jh, [P, PACK * JH], BF16) for jh in range(2)]
+        xb_rows = tile("xb_rows", [P, PACK, JH], BF16, tag="root1")
         for t in range(PACK):
             nc.scalar.activation(xb_rows[:, t, :], gb[:, t, JH:], ACT.Copy, scale=tail_sb[:, t : t + 1])
         nc.scalar.copy(out=woven(xb_bf[1]), in_=by_line(xb_rows, 0))
@@ -260,33 +267,33 @@ def tile_list_tracer_release_scores_kernel(
         xb_q.append(quantized("xb1", xb_bf[1]))
         xa_q.append(quantized("xa1", xa_bf[1]))
 
-        def score(kind, half, pair, b):
-            ps = bank(b, "y%s%d_%d" % (kind, half, pair))
+        def score(kind, jh, pair, b):
+            ps = bank(b, "y%s%d_%d" % (kind, jh, pair))
             for e in range(2):
                 n = 2 * pair + e
                 cols = slice(P * n, P * (n + 1))
                 if kind == "a":
-                    lhsT, lhsT_scale, (codes, scales) = wa_q[:, cols].bitcast(FP8X4), wa_sc[:, cols], xa_q[half]
+                    lhsT, lhsT_scale, (codes, scales) = wa_q[:, cols].bitcast(FP8X4), wa_sc[:, cols], xa_q[jh]
                 else:
-                    lhsT, lhsT_scale, (codes, scales) = wb_w[:, 2 * P * n : 2 * P * (n + 1)].bitcast(FP4X4), wb_sc[:, cols], xb_q[half]
+                    lhsT, lhsT_scale, (codes, scales) = wb_w[:, 2 * P * n : 2 * P * (n + 1)].bitcast(FP4X4), wb_sc[:, cols], xb_q[jh]
                 nc.tensor.matmul_mx(
                     ps[:, JH * e : JH * (e + 1)], lhsT=lhsT, lhsT_scale=lhsT_scale,
                     rhs=codes[:].bitcast(FP8X4), rhs_scale=scales[:], start=True, stop=True,
                 )
             return ps
 
-        for half in range(2):
+        for jh in range(2):
             yb_sb = []
             for pair in range(3):
-                yb_ps = score("b", half, pair, (6 * half + pair) % 8)
-                copied = tile("yb_sb%d_%d" % (half, pair), [P, BANK], F32)
+                yb_ps = score("b", jh, pair, (6 * jh + pair) % 8)
+                copied = tile("yb_sb%d_%d" % (jh, pair), [P, BANK], F32)
                 nc.scalar.copy(out=copied[:], in_=yb_ps[:])
                 yb_sb.append(copied)
             for pair in range(3):
-                ya_ps = score("a", half, pair, (6 * half + 3 + pair) % 8)
-                res = tile("res%d_%d" % (half, pair), [P, BANK], F32)
+                ya_ps = score("a", jh, pair, (6 * jh + 3 + pair) % 8)
+                res = tile("res%d_%d" % (jh, pair), [P, BANK], F32)
                 nc.vector.tensor_tensor(out=res[:], in0=ya_ps[:], in1=yb_sb[pair][:], op=ALU.max)
                 nc.sync.dma_start(
-                    out[2 * P * pair : 2 * P * (pair + 1), JH * half : JH * (half + 1)].rearrange("(e p) j -> p e j", p=P),
+                    out[2 * P * pair : 2 * P * (pair + 1), JH * jh : JH * (jh + 1)].rearrange("(e p) j -> p e j", p=P),
                     res[:].rearrange("p (e j) -> p e j", e=2),
                 )

@@ -46,9 +46,9 @@ def tile_list_tracer_release_scores_kernel(
         w4_sc_raw = tile("w4_sc_raw", [P, H], U8)
         wb_sc = tile("wb_sc", [P, N], U8)
         v2_sc = tile("v2_sc", [P, S], U8)
-        for plane in (tab_sc, v2_sc):
+        for plane in (tab_sc, w4_sc_raw):
             nc.vector.memset(plane[:].bitcast(I32), 0)
-        for plane in (wd_sc_raw, w4_sc_raw, wb_sc):
+        for plane in (wd_sc_raw, v2_sc, wb_sc):
             nc.gpsimd.memset(plane[:].bitcast(I32), 0)
 
         def load_tab(a, **place):
@@ -81,16 +81,16 @@ def tile_list_tracer_release_scores_kernel(
         nc.sync.dma_start(wd_raw[:], wd_words.rearrange("a p c i -> p a (c i)").bitcast(I32))
         nc.sync.dma_start(p2[:], pos2)
         tab1 = load_tab(1)
-        w1_raw0 = load_w1(0)
-        tab2 = load_tab(2, offset=0)
-        w1_raw1 = load_w1(1)
+        w1_raw0 = load_w1(0, offset=8 * T)
+        tab2 = load_tab(2)
+        w1_raw1 = load_w1(1, offset=14 * T)
         load_scale_rows(nc.scalar, tab_sc, 0, tab_scales)
         load_scale_rows(nc.gpsimd, wd_sc_raw, 0, wd_scales)
         ones = tile("ones", [P, 1], F32)
         warm = tile("warm", [P, 1], F32)
         nc.gpsimd.memset(ones[:], 1.0)
         nc.scalar.activation(warm[:], ones[:], ACT.Abs_reciprocal_sqrt)
-        load_scale_rows(nc.gpsimd, w4_sc_raw, 0, w4_scales)
+        load_scale_rows(nc.scalar, w4_sc_raw, 0, w4_scales)
         load_scale_rows(nc.gpsimd, wb_sc, 0, wb_scales)
 
         w4_w = tile("w4_w", [P, 2 * H], U8)
@@ -150,30 +150,31 @@ def tile_list_tracer_release_scores_kernel(
             )
 
         d_ps = {0: banks(0, "d0"), 1: banks(1, "d1")}
-        for t in range(2):
+        for a in range(PASSES):
             for h in range(2):
-                for a in range(PASSES):
+                for t in range(2):
                     d_pass(d_ps[t], t, h, a)
 
-        w1_q = [tile("w1_q0", [P, H], U32, offset=0), tile("w1_q1", [P, H], U32)]
+        w1_q = [tile("w1_q%d" % g, [P, H], U32) for g in range(2)]
         w1_sc = [tile("w1_sc%d" % g, [P, H], U8) for g in range(2)]
-        w1_bf = [tile("w1_bf%d" % g, [P, PACK * H], BF16) for g in range(2)]
+        w1_bf = [tile("w1_bf0", [P, PACK * H], BF16), tile("w1_bf1", [P, PACK * H], BF16, offset=8 * T)]
         for g, (copy, raw) in enumerate(((nc.scalar.copy, w1_raw0), (nc.vector.tensor_copy, w1_raw1))):
             copy(
                 w1_bf[g][:].rearrange("p (t m j) -> p m j t", t=PACK, j=PACK),
                 raw[:].rearrange("p j (m t) -> p m j t", t=PACK),
             )
-        w4_sc = deal_scales("w4_sc", w4_sc_raw, offset=4 * H)
-        base_sb = tile("base_sb", [P, PACK, J], F32, tag="w1_raw0")
-        nc.sync.dma_start(base_sb[:], base.rearrange("(p t) j -> p t j", t=PACK))
-        tail_sb = tile("tail_sb", [P, PACK], F32, tag="w1_raw1")
-        nc.sync.dma_start(tail_sb[:], tail.rearrange("(p t) -> p t", t=PACK))
-        wb_w = tile("wb_w", [P, 2 * N], U8, tag="w4_sc_raw")
-        nc.sync.dma_start(wb_w[:].bitcast(I32), wb_words[0].bitcast(I32))
-        nc.vector.quantize_mx(out=w1_q[0][:].bitcast(FP8X4), scales=w1_sc[0][:], in_=w1_bf[0][:])
         for t in range(PACK):
             cols = slice(P * t, P * (t + 1))
-            nc.vector.quantize_mx(out=w1_q[1][:, cols].bitcast(FP8X4), scales=w1_sc[1][:, cols], in_=w1_bf[1][:, H * t : H * (t + 1)])
+            for g in range(2):
+                nc.vector.quantize_mx(out=w1_q[g][:, cols].bitcast(FP8X4), scales=w1_sc[g][:, cols], in_=w1_bf[g][:, H * t : H * (t + 1)])
+            if t == 0:
+                w4_sc = deal_scales("w4_sc", w4_sc_raw, offset=14 * T)
+        base_sb = tile("base_sb", [P, PACK, J], F32, offset=10 * T)
+        nc.sync.dma_start(base_sb[:], base.rearrange("(p t) j -> p t j", t=PACK))
+        tail_sb = tile("tail_sb", [P, PACK], F32, offset=15 * T)
+        nc.sync.dma_start(tail_sb[:], tail.rearrange("(p t) -> p t", t=PACK))
+        wb_w = tile("wb_w", [P, 2 * N], U8, offset=16 * T)
+        nc.sync.dma_start(wb_w[:].bitcast(I32), wb_words[0].bitcast(I32))
 
         def d_sum(t, pair):
             d_ps[t] = banks(pair, "d%d" % t)
@@ -204,7 +205,8 @@ def tile_list_tracer_release_scores_kernel(
 
         ga = tile("ga", [P, PACK, J], F32)
         gb = tile("gb", [P, PACK, J], F32)
-        a_pair = (2, 1, 2, 1)
+        a_pair = (2, 0, 2, 0)
+        d_pair = (0, 1, 1, 1)
         for t in range(PACK):
             mag = [sb.tile([P, BANK], F32, name="mag", bufs=4) for h in range(2)]
             root = [tile("root%d_%d" % (t, h), [P, BANK], F32, tag="root%d" % h) for h in range(2)]
@@ -216,8 +218,8 @@ def tile_list_tracer_release_scores_kernel(
             for h in range(2):
                 nc.scalar.activation(damp[h][:], root[h][:], ACT.Square)
             a_ps = a_sum(t, a_pair[t])
-            if t in (0, 2):
-                d_sum(t // 2 + 2, 0)
+            if t in (1, 2):
+                d_sum(t + 1, d_pair[t + 1])
             h_sb = tile("h%d" % t, [P, S], F32)
             for h in range(2):
                 nc.vector.scalar_tensor_tensor(

@@ -80,6 +80,8 @@ def tile_list_tracer_release_scores_kernel(
         wd_raw = tile("wd_raw", [P, PASSES, H], I32, offset=4 * T)
         nc.sync.dma_start(wd_raw[:], wd_words.rearrange("a p c i -> p a (c i)").bitcast(I32))
         nc.sync.dma_start(p2[:], pos2)
+        tail_sb = tile("tail_sb", [P, PACK], F32)
+        nc.sync.dma_start(tail_sb[:], tail.rearrange("(p t) -> p t", t=PACK))
         tab1 = load_tab(1)
         w1_raw0 = load_w1(0, offset=8 * T)
         tab2 = load_tab(2)
@@ -92,11 +94,13 @@ def tile_list_tracer_release_scores_kernel(
         nc.scalar.activation(warm[:], ones[:], ACT.Abs_reciprocal_sqrt)
         load_scale_rows(nc.scalar, w4_sc_raw, 0, w4_scales)
         load_scale_rows(nc.gpsimd, wb_sc, 0, wb_scales)
+        tail_rows = tile("tail_rows", [P, PACK, J], F32)
+        nc.scalar.copy(out=tail_rows[:], in_=tail_sb[:].unsqueeze(2).to_broadcast([P, PACK, J]))
 
         w4_w = tile("w4_w", [P, 2 * H], U8)
         nc.vector.tensor_copy(
-            out=w4_w[:].rearrange("p (t m b) -> p m t b", t=PACK, b=2),
-            in_=w4_raw[:].rearrange("p (m t b) -> p m t b", t=PACK, b=2),
+            out=w4_w[:].rearrange("p (t m b) -> p t m b", t=PACK, b=2),
+            in_=w4_raw[:].rearrange("p (m t b) -> p t m b", t=PACK, b=2),
         )
 
         half_cols = BANK // 16
@@ -113,8 +117,8 @@ def tile_list_tracer_release_scores_kernel(
         def deal_scales(name, raw, **place):
             dealt = tile(name, [P, H], U8, **place)
             nc.vector.tensor_copy(
-                out=dealt[:].rearrange("p (t m) -> p m t", t=PACK),
-                in_=raw[:].rearrange("p (m t) -> p m t", t=PACK),
+                out=dealt[:].rearrange("p (t m) -> p t m", t=PACK),
+                in_=raw[:].rearrange("p (m t) -> p t m", t=PACK),
             )
             return dealt
 
@@ -126,13 +130,13 @@ def tile_list_tracer_release_scores_kernel(
         )
         v_sc = gather_table("v_sc", tab_sc[:], U8, offset=4 * T + H)
         for q in range(4):
-            nc.scalar.dma_start(v2_sc[32 * q : 32 * q + 4, :].bitcast(I32), v_sc[32 * q + 8 : 32 * q + 12, :].bitcast(I32))
+            nc.sync.dma_start(v2_sc[32 * q : 32 * q + 4, :].bitcast(I32), v_sc[32 * q + 8 : 32 * q + 12, :].bitcast(I32))
         gain_sb = tile("gain_sb", [P, PACK], F32, tag="tab_sc")
         nc.sync.dma_start(gain_sb[:], gain.rearrange("(p t) -> p t", t=PACK))
         wd_sc = deal_scales("wd_sc", wd_sc_raw, offset=4 * T)
         v_w.append(gather_table("v1", tab1[:].bitcast(U32), U32, tag="wd_sc_raw"))
-        wa_raw = tile("wa_raw", [P, PACK, N], F32, tag="tab1")
-        nc.sync.dma_start(wa_raw[:], wa.rearrange("(p j) n -> p j n", j=PACK))
+        base_sb = tile("base_sb", [P, PACK, J], F32, tag="tab1")
+        nc.sync.dma_start(base_sb[:], base.rearrange("(p t) j -> p t j", t=PACK))
         v_w.append(gather_table("v2", tab2[:].bitcast(U32), U32))
 
         def bank(b, name):
@@ -169,10 +173,8 @@ def tile_list_tracer_release_scores_kernel(
                 nc.vector.quantize_mx(out=w1_q[g][:, cols].bitcast(FP8X4), scales=w1_sc[g][:, cols], in_=w1_bf[g][:, H * t : H * (t + 1)])
             if t == 0:
                 w4_sc = deal_scales("w4_sc", w4_sc_raw, offset=14 * T)
-        base_sb = tile("base_sb", [P, PACK, J], F32, offset=10 * T)
-        nc.sync.dma_start(base_sb[:], base.rearrange("(p t) j -> p t j", t=PACK))
-        tail_sb = tile("tail_sb", [P, PACK], F32, offset=15 * T)
-        nc.sync.dma_start(tail_sb[:], tail.rearrange("(p t) -> p t", t=PACK))
+        wa_raw = tile("wa_raw", [P, PACK, N], F32, tag="tab2")
+        nc.sync.dma_start(wa_raw[:], wa.rearrange("(p j) n -> p j n", j=PACK))
         wb_w = tile("wb_w", [P, 2 * N], U8, offset=16 * T)
         nc.sync.dma_start(wb_w[:].bitcast(I32), wb_words[0].bitcast(I32))
 
@@ -226,8 +228,8 @@ def tile_list_tracer_release_scores_kernel(
                     out=h_sb[:, h * BANK : (h + 1) * BANK], in0=a_ps[h][:], scalar=gain_sb[:, t : t + 1],
                     in1=damp[h][:], op0=ALU.mult, op1=ALU.mult,
                 )
-            nc.vector.tensor_copy(gb[:, t, :], h_sb[:].indirect(p2[:]))
-            nc.vector.tensor_copy(ga[:, t, :], h_sb[:].indirect(p1[:]))
+            nc.vector.tensor_tensor(gb[:, t, :], h_sb[:].indirect(p2[:]), tail_rows[:, t, :], ALU.mult)
+            nc.vector.tensor_tensor(ga[:, t, :], h_sb[:].indirect(p1[:]), base_sb[:, t, :], ALU.add)
 
         wa_bf = tile("wa_bf", [P, PACK * N], BF16, tag="root0")
         wa_q = tile("wa_q", [P, N], U32)
@@ -254,20 +256,13 @@ def tile_list_tracer_release_scores_kernel(
 
         xa_bf = [tile("xa_bf%d" % jh, [P, PACK * JH], BF16) for jh in range(2)]
         xb_bf = [tile("xb_bf%d" % jh, [P, PACK * JH], BF16) for jh in range(2)]
-        xb_rows = tile("xb_rows", [P, PACK, JH], BF16, tag="root1")
-        for t in range(PACK):
-            nc.scalar.activation(xb_rows[:, t, :], gb[:, t, JH:], ACT.Copy, scale=tail_sb[:, t : t + 1])
-        nc.scalar.copy(out=woven(xb_bf[1]), in_=by_line(xb_rows, 0))
-        nc.vector.tensor_tensor(
-            out=woven(xb_bf[0]), in0=by_line(gb, 0),
-            in1=tail_sb[:].unsqueeze(1).unsqueeze(3).to_broadcast([P, JH // 4, PACK, 4]), op=ALU.mult,
-        )
-        nc.vector.tensor_tensor(out=woven(xa_bf[0]), in0=by_line(ga, 0), in1=by_line(base_sb, 0), op=ALU.add)
-        xb_q = [quantized("xb0", xb_bf[0])]
-        xa_q = [quantized("xa0", xa_bf[0])]
-        nc.vector.tensor_tensor(out=woven(xa_bf[1]), in0=by_line(ga, 1), in1=by_line(base_sb, 1), op=ALU.add)
-        xb_q.append(quantized("xb1", xb_bf[1]))
-        xa_q.append(quantized("xa1", xa_bf[1]))
+        for jh, copy in enumerate((nc.vector.tensor_copy, nc.scalar.copy)):
+            copy(woven(xb_bf[jh]), by_line(gb, jh))
+            copy(woven(xa_bf[jh]), by_line(ga, jh))
+        xa_q, xb_q = [], []
+        for jh in range(2):
+            xb_q.append(quantized("xb%d" % jh, xb_bf[jh]))
+            xa_q.append(quantized("xa%d" % jh, xa_bf[jh]))
 
         def score(kind, jh, pair, b):
             ps = bank(b, "y%s%d_%d" % (kind, jh, pair))
@@ -285,16 +280,14 @@ def tile_list_tracer_release_scores_kernel(
             return ps
 
         for jh in range(2):
-            yb_sb = []
             for pair in range(3):
-                yb_ps = score("b", jh, pair, (6 * jh + pair) % 8)
-                copied = tile("yb_sb%d_%d" % (jh, pair), [P, BANK], F32)
-                nc.scalar.copy(out=copied[:], in_=yb_ps[:])
-                yb_sb.append(copied)
-            for pair in range(3):
-                ya_ps = score("a", jh, pair, (6 * jh + 3 + pair) % 8)
-                res = tile("res%d_%d" % (jh, pair), [P, BANK], F32)
-                nc.vector.tensor_tensor(out=res[:], in0=ya_ps[:], in1=yb_sb[pair][:], op=ALU.max)
+                step = 3 * jh + pair
+                yb_ps = score("b", jh, pair, (2 * step) % 8)
+                yb_sb = tile("yb_sb%d" % step, [P, BANK], F32)
+                nc.scalar.copy(out=yb_sb[:], in_=yb_ps[:])
+                ya_ps = score("a", jh, pair, (2 * step + 1) % 8)
+                res = tile("res%d" % step, [P, BANK], F32)
+                nc.vector.tensor_tensor(out=res[:], in0=ya_ps[:], in1=yb_sb[:], op=ALU.max)
                 nc.sync.dma_start(
                     out[2 * P * pair : 2 * P * (pair + 1), JH * jh : JH * (jh + 1)].rearrange("(e p) j -> p e j", p=P),
                     res[:].rearrange("p (e j) -> p e j", e=2),

from contextlib import ExitStack

import concourse.mybir as mybir

F32 = mybir.dt.float32
BF16 = mybir.dt.bfloat16
I32 = mybir.dt.int32
U32 = mybir.dt.uint32
U16 = mybir.dt.uint16
U8 = mybir.dt.uint8
FP8X4 = mybir.dt.float8_e4m3fn_x4
FP4X4 = mybir.dt.float4_e2m1fn_x4
ACT = mybir.ActivationFunctionType
ALU = mybir.AluOpType

P = 128
PACK = 4
T = 2048
S = 1024
H = 512
J = 512
N = 768
BANK = 512
PASSES = 3
JH = J // 2
FLOPS = 2 * (2 * 1536 * H * S + 2 * H * N * J)


def tile_list_tracer_release_scores_kernel(
    tc, tab_words, tab_scales, offs, pos1, pos2, w1, w4_words, w4_scales,
    wd_words, wd_scales, gain, base, tail, wa, wb_words, wb_scales, out,
):
    nc = tc.nc
    with ExitStack() as ctx:
        sb = ctx.enter_context(tc.tile_pool(name="sb", bufs=1))
        shared = ctx.enter_context(tc.tile_pool(name="shared", bufs=1))
        psum = ctx.enter_context(tc.psum_pool(name="psum", bufs=1))

        def tile(name, shape, dtype, tag=None, offset=None):
            if offset is not None:
                return shared.tile(shape, dtype, name=name, align_bytes=64, offset=offset)
            return sb.tile(shape, dtype, name=name, tag=tag or name, align_bytes=64)

        tab_sc = tile("tab_sc", [P, T], U8)
        wd_sc_raw = tile("wd_sc_raw", [P, H], U8)
        w4_sc_raw = tile("w4_sc_raw", [P, H], U8)
        wb_sc = tile("wb_sc", [P, N], U8)
        v2_sc = tile("v2_sc", [P, S], U8)
        for plane in (tab_sc, w4_sc_raw):
            nc.vector.memset(plane[:].bitcast(I32), 0)
        for plane in (wd_sc_raw, v2_sc, wb_sc):
            nc.gpsimd.memset(plane[:].bitcast(I32), 0)

        def load_tab(a, **place):
            words = tile("tab%d" % a, [P, T], I32, **place)
            nc.sync.dma_start(words[:], tab_words[a].rearrange("p t i -> p (t i)").bitcast(I32))
            return words

        def load_w1(g, **place):
            raw = tile("w1_raw%d" % g, [P, PACK, H], F32, **place)
            nc.sync.dma_start(raw[:], w1[512 * g : 512 * (g + 1), :].rearrange("(p j) c -> p j c", j=PACK))
            return raw

        def load_scale_rows(engine, plane, first, scales):
            rows = 4 * scales.shape[0]
            for q in range(4):
                engine.dma_start(
                    plane[32 * q + first : 32 * q + first + rows, :].bitcast(I32),
                    scales.bitcast(I32)[:, 4 * q : 4 * q + 4, :],
                )

        idx = sb.tile([P, S // 16], U16, name="idx")
        p1 = sb.tile([P, J // 16], U16, name="p1")
        p2 = sb.tile([P, J // 16], U16, name="p2")
        w4_raw = tile("w4_raw", [P, 2 * H], U8)
        nc.sync.dma_start(w4_raw[:].bitcast(I32), w4_words[0].bitcast(I32))
        tab0 = load_tab(0)
        nc.sync.dma_start(idx[:], offs)
        nc.sync.dma_start(p1[:], pos1)
        wd_raw = tile("wd_raw", [P, PASSES, H], I32, offset=4 * T)
        nc.sync.dma_start(wd_raw[:], wd_words.rearrange("a p c i -> p a (c i)").bitcast(I32))
        nc.sync.dma_start(p2[:], pos2)
        tail_sb = tile("tail_sb", [P, PACK], F32)
        nc.sync.dma_start(tail_sb[:], tail.rearrange("(p t) -> p t", t=PACK))
        tab1 = load_tab(1)
        w1_raw0 = load_w1(0, offset=8 * T)
        tab2 = load_tab(2)
        w1_raw1 = load_w1(1, offset=14 * T)
        load_scale_rows(nc.scalar, tab_sc, 0, tab_scales)
        load_scale_rows(nc.gpsimd, wd_sc_raw, 0, wd_scales)
        ones = tile("ones", [P, 1], F32)
        warm = tile("warm", [P, 1], F32)
        nc.gpsimd.memset(ones[:], 1.0)
        nc.scalar.activation(warm[:], ones[:], ACT.Abs_reciprocal_sqrt)
        load_scale_rows(nc.scalar, w4_sc_raw, 0, w4_scales)
        load_scale_rows(nc.gpsimd, wb_sc, 0, wb_scales)
        tail_rows = tile("tail_rows", [P, PACK, J], F32)
        nc.scalar.copy(out=tail_rows[:], in_=tail_sb[:].unsqueeze(2).to_broadcast([P, PACK, J]))

        w4_w = tile("w4_w", [P, 2 * H], U8)
        nc.vector.tensor_copy(
            out=w4_w[:].rearrange("p (t m b) -> p t m b", t=PACK, b=2),
            in_=w4_raw[:].rearrange("p (m t b) -> p t m b", t=PACK, b=2),
        )

        half_cols = BANK // 16

        def half(h):
            return slice(h * BANK, (h + 1) * BANK)

        def gather_table(name, window, dtype, **place):
            picked = tile(name, [P, S], dtype, **place)
            for h in range(2):
                nc.vector.tensor_copy(picked[:, half(h)], window.indirect(idx[:, h * half_cols : (h + 1) * half_cols]))
            return picked

        def deal_scales(name, raw, **place):
            dealt = tile(name, [P, H], U8, **place)
            nc.vector.tensor_copy(
                out=dealt[:].rearrange("p (t m) -> p t m", t=PACK),
                in_=raw[:].rearrange("p (m t) -> p t m", t=PACK),
            )
            return dealt

        v_w = [gather_table("v0", tab0[:].bitcast(U32), U32)]
        wd_w = tile("wd_w", [P, PASSES, H], I32)
        nc.vector.tensor_copy(
            out=wd_w[:].rearrange("p a (t u i) -> p a u t i", t=PACK, i=4),
            in_=wd_raw[:].rearrange("p a (u i t) -> p a u t i", t=PACK, i=4),
        )
        v_sc = gather_table("v_sc", tab_sc[:], U8, offset=4 * T + H)
        for q in range(4):
            nc.sync.dma_start(v2_sc[32 * q : 32 * q + 4, :].bitcast(I32), v_sc[32 * q + 8 : 32 * q + 12, :].bitcast(I32))
        gain_sb = tile("gain_sb", [P, PACK], F32, tag="tab_sc")
        nc.sync.dma_start(gain_sb[:], gain.rearrange("(p t) -> p t", t=PACK))
        wd_sc = deal_scales("wd_sc", wd_sc_raw, offset=4 * T)
        v_w.append(gather_table("v1", tab1[:].bitcast(U32), U32, tag="wd_sc_raw"))
        base_sb = tile("base_sb", [P, PACK, J], F32, tag="tab1")
        nc.sync.dma_start(base_sb[:], base.rearrange("(p t) j -> p t j", t=PACK))
        v_w.append(gather_table("v2", tab2[:].bitcast(U32), U32))

        def bank(b, name):
            return psum.tile([P, BANK], F32, name=name, tag="bank%d" % b)

        def banks(pair, name):
            return [bank(2 * pair + h, "%s_%d" % (name, h)) for h in range(2)]

        def d_pass(ps, t, h, a):
            cols = slice(P * t, P * (t + 1))
            nc.tensor.matmul_mx(
                ps[h][:], lhsT=wd_w[:, a, cols].bitcast(FP8X4), lhsT_scale=wd_sc[4 * a :, cols],
                rhs=v_w[a][:, half(h)].bitcast(FP8X4), rhs_scale=v_sc[4 * a :, half(h)],
                start=(a == 0), stop=(a == PASSES - 1),
            )

        d_ps = {0: banks(0, "d0"), 1: banks(1, "d1")}
        for a in range(PASSES):
            for h in range(2):
                for t in range(2):
                    d_pass(d_ps[t], t, h, a)

        w1_q = [tile("w1_q%d" % g, [P, H], U32) for g in range(2)]
        w1_sc = [tile("w1_sc%d" % g, [P, H], U8) for g in range(2)]
        w1_bf = [tile("w1_bf0", [P, PACK * H], BF16), tile("w1_bf1", [P, PACK * H], BF16, offset=8 * T)]
        for g, (copy, raw) in enumerate(((nc.scalar.copy, w1_raw0), (nc.vector.tensor_copy, w1_raw1))):
            copy(
                w1_bf[g][:].rearrange("p (t m j) -> p m j t", t=PACK, j=PACK),
                raw[:].rearrange("p j (m t) -> p m j t", t=PACK),
            )
        for t in range(PACK):
            cols = slice(P * t, P * (t + 1))
            for g in range(2):
                nc.vector.quantize_mx(out=w1_q[g][:, cols].bitcast(FP8X4), scales=w1_sc[g][:, cols], in_=w1_bf[g][:, H * t : H * (t + 1)])
            if t == 0:
                w4_sc = deal_scales("w4_sc", w4_sc_raw, offset=14 * T)
        wa_raw = tile("wa_raw", [P, PACK, N], F32, tag="tab2")
        nc.sync.dma_start(wa_raw[:], wa.rearrange("(p j) n -> p j n", j=PACK))
        wb_w = tile("wb_w", [P, 2 * N], U8, offset=16 * T)
        nc.sync.dma_start(wb_w[:].bitcast(I32), wb_words[0].bitcast(I32))

        def d_sum(t, pair):
            d_ps[t] = banks(pair, "d%d" % t)
            for h in range(2):
                for a in range(PASSES):
                    d_pass(d_ps[t], t, h, a)

        def a_sum(t, pair):
            cols = slice(P * t, P * (t + 1))
            ps = banks(pair, "a%d" % t)

            def w1_pass(g, h):
                nc.tensor.matmul_mx(
                    ps[h][:], lhsT=w1_q[g][:, cols].bitcast(FP8X4), lhsT_scale=w1_sc[g][:, cols],
                    rhs=v_w[g][:, half(h)].bitcast(FP8X4), rhs_scale=v_sc[4 * g :, half(h)],
                    start=(g == 0), stop=False,
                )

            for h in range(2):
                w1_pass(0, h)
                w1_pass(1, h)
                nc.tensor.matmul_mx(
                    ps[h][:], lhsT=w4_w[:, 2 * P * t : 2 * P * (t + 1)].bitcast(FP4X4), lhsT_scale=w4_sc[:, cols],
                    rhs=v_w[2][:, half(h)].bitcast(FP8X4), rhs_scale=v2_sc[:, half(h)],
                    start=False, stop=True,
                )
            return ps

        ga = tile("ga", [P, PACK, J], F32)
        gb = tile("gb", [P, PACK, J], F32)
        a_pair = (2, 0, 2, 0)
        d_pair = (0, 1, 1, 1)
        for t in range(PACK):
            mag = [sb.tile([P, BANK], F32, name="mag", bufs=4) for h in range(2)]
            root = [tile("root%d_%d" % (t, h), [P, BANK], F32, tag="root%d" % h) for h in range(2)]
            damp = [tile("damp%d_%d" % (t, h), [P, BANK], F32) for h in range(2)]
            for h in range(2):
                nc.scalar.activation(mag[h][:], d_ps[t][h][:], ACT.Abs)
            for h in range(2):
                nc.scalar.activation(root[h][:], mag[h][:], ACT.Abs_reciprocal_sqrt, bias=1.0)
            for h in range(2):
                nc.scalar.activation(damp[h][:], root[h][:], ACT.Square)
            a_ps = a_sum(t, a_pair[t])
            if t in (1, 2):
                d_sum(t + 1, d_pair[t + 1])
            h_sb = tile("h%d" % t, [P, S], F32)
            for h in range(2):
                nc.vector.scalar_tensor_tensor(
                    out=h_sb[:, h * BANK : (h + 1) * BANK], in0=a_ps[h][:], scalar=gain_sb[:, t : t + 1],
                    in1=damp[h][:], op0=ALU.mult, op1=ALU.mult,
                )
            nc.vector.tensor_tensor(gb[:, t, :], h_sb[:].indirect(p2[:]), tail_rows[:, t, :], ALU.mult)
            nc.vector.tensor_tensor(ga[:, t, :], h_sb[:].indirect(p1[:]), base_sb[:, t, :], ALU.add)

        wa_bf = tile("wa_bf", [P, PACK * N], BF16, tag="root0")
        wa_q = tile("wa_q", [P, N], U32)
        wa_sc = tile("wa_sc", [P, N], U8)
        for c0 in range(0, N, 256):
            nc.scalar.copy(
                out=wa_bf[:, PACK * c0 : PACK * (c0 + 256)].rearrange("p (c i j) -> p c j i", i=4, j=PACK),
                in_=wa_raw[:, :, c0 : c0 + 256].rearrange("p j (c i) -> p c j i", i=4),
            )
        for c0 in range(0, N, 256):
            nc.vector.quantize_mx(out=wa_q[:, c0 : c0 + 256].bitcast(FP8X4), scales=wa_sc[:, c0 : c0 + 256], in_=wa_bf[:, PACK * c0 : PACK * (c0 + 256)])

        def woven(x):
            return x[:].rearrange("p (c i t) -> p c t i", i=4, t=PACK)

        def by_line(x, jh):
            return x[:, :, JH * jh : JH * (jh + 1)].rearrange("p t (c i) -> p c t i", i=4)

        def quantized(name, x_bf):
            codes = tile(name + "_q", [P, JH], U32)
            scales = tile(name + "_sc", [P, JH], U8)
            nc.vector.quantize_mx(out=codes[:].bitcast(FP8X4), scales=scales[:], in_=x_bf[:])
            return codes, scales

        xa_bf = [tile("xa_bf%d" % jh, [P, PACK * JH], BF16) for jh in range(2)]
        xb_bf = [tile("xb_bf%d" % jh, [P, PACK * JH], BF16) for jh in range(2)]
        for jh, copy in enumerate((nc.vector.tensor_copy, nc.scalar.copy)):
            copy(woven(xb_bf[jh]), by_line(gb, jh))
            copy(woven(xa_bf[jh]), by_line(ga, jh))
        xa_q, xb_q = [], []
        for jh in range(2):
            xb_q.append(quantized("xb%d" % jh, xb_bf[jh]))
            xa_q.append(quantized("xa%d" % jh, xa_bf[jh]))

        def score(kind, jh, pair, b):
            ps = bank(b, "y%s%d_%d" % (kind, jh, pair))
            for e in range(2):
                n = 2 * pair + e
                cols = slice(P * n, P * (n + 1))
                if kind == "a":
                    lhsT, lhsT_scale, (codes, scales) = wa_q[:, cols].bitcast(FP8X4), wa_sc[:, cols], xa_q[jh]
                else:
                    lhsT, lhsT_scale, (codes, scales) = wb_w[:, 2 * P * n : 2 * P * (n + 1)].bitcast(FP4X4), wb_sc[:, cols], xb_q[jh]
                nc.tensor.matmul_mx(
                    ps[:, JH * e : JH * (e + 1)], lhsT=lhsT, lhsT_scale=lhsT_scale,
                    rhs=codes[:].bitcast(FP8X4), rhs_scale=scales[:], start=True, stop=True,
                )
            return ps

        for jh in range(2):
            for pair in range(3):
                step = 3 * jh + pair
                yb_ps = score("b", jh, pair, (2 * step) % 8)
                yb_sb = tile("yb_sb%d" % step, [P, BANK], F32)
                nc.scalar.copy(out=yb_sb[:], in_=yb_ps[:])
                ya_ps = score("a", jh, pair, (2 * step + 1) % 8)
                res = tile("res%d" % step, [P, BANK], F32)
                nc.vector.tensor_tensor(out=res[:], in0=ya_ps[:], in1=yb_sb[:], op=ALU.max)
                nc.sync.dma_start(
                    out[2 * P * pair : 2 * P * (pair + 1), JH * jh : JH * (jh + 1)].rearrange("(e p) j -> p e j", p=P),
                    res[:].rearrange("p (e j) -> p e j", e=2),
                )
